import numpy as np
import ml_dtypes


def mxq(x, axis, fmt="e4m3"):
    dtype, down = {"e4m3": (ml_dtypes.float8_e4m3fn, 7), "e5m2": (ml_dtypes.float8_e5m2, 14)}[fmt]
    v = np.moveaxis(np.asarray(x, np.float32).astype(ml_dtypes.bfloat16).astype(np.float64), axis, -1)
    blocks = v.reshape(v.shape[:-1] + (-1, 32))
    amax = np.abs(blocks).max(-1, keepdims=True)
    byte = np.maximum(np.where(amax > 0, np.frexp(amax)[1] - 1 + 127, 0) - down, 1)
    scale = np.exp2(byte - 127.0)
    codes = (blocks / scale).astype(np.float32).astype(dtype).astype(np.float64)
    return np.moveaxis((codes * scale).reshape(v.shape), -1, axis)


WIDE = False


def mx_kscale(k):
    if not WIDE:
        return np.ones(k)
    levels = np.array([10, -10, 5, -5, 0])
    if k % 512:
        return np.exp2(np.random.permutation(np.resize(levels, k // 32))).repeat(32)
    a = np.empty((k // 512, 16))
    for p in range(k // 512):
        a[p, :8] = np.random.permutation(np.resize(levels, 8))
        for g in range(8):
            far = levels[np.abs(levels - a[p, g]) >= 10]
            a[p, g + 8] = far[np.random.randint(len(far))]
    return np.exp2(a.ravel()).repeat(32)


def f64(x):
    return np.asarray(x).astype(np.float64)


def striped(idx):
    return np.tile(np.asarray(idx).reshape(-1, 16).T, (8, 1)).astype(np.uint16)


def unstriped(offs):
    return offs[:16].T.reshape(-1).astype(np.int64)


E2M1 = np.array([0.0, 0.5, 1.0, 1.5, 2.0, 3.0, 4.0, 6.0, -0.0, -0.5, -1.0, -1.5, -2.0, -3.0, -4.0, -6.0])


def pack_weight(w, fmt):
    k, n = w.shape
    w = f64(np.asarray(w, np.float32).astype(ml_dtypes.bfloat16)).reshape(k // 32, 32, n)
    amax = np.abs(w).max(1)
    if fmt == "e4m3":
        byte = np.frexp(amax)[1] - 1 + 127 - 7
    else:
        mant, ex = np.frexp(amax / 6.0)
        byte = np.where(mant > 0.5, ex, ex - 1) + 127
    byte = np.clip(np.where(amax > 0, byte, 1), 1, 254)
    scaled = (w * np.exp2(127.0 - byte)[:, None, :]).reshape(k, n).astype(np.float32)
    by_word = np.ascontiguousarray(scaled.reshape(k // 512, 128, 4, n).transpose(0, 1, 3, 2))
    if fmt == "e4m3":
        words = by_word.astype(ml_dtypes.float8_e4m3fn).view(np.uint8)
    else:
        c = by_word.astype(ml_dtypes.float4_e2m1fn).view(np.uint8) & 0xF
        words = (c[..., 0::2] | (c[..., 1::2] << 4)).reshape(k // 512, 128, 2 * n)
    return np.ascontiguousarray(words), np.ascontiguousarray(byte.astype(np.uint8).reshape(k // 512, 16, n))


def unpack_weight(words, scales, fmt):
    g, _, n = scales.shape
    words = np.ascontiguousarray(words).reshape(g, 128, n, -1)
    if fmt == "e4m3":
        vals = words.view(ml_dtypes.float8_e4m3fn).astype(np.float64)
    else:
        nib = np.empty((g, 128, n, 4), np.uint8)
        nib[..., 0::2] = words & 0xF
        nib[..., 1::2] = words >> 4
        vals = E2M1[nib]
    vals = vals * np.repeat(np.exp2(scales.astype(np.float64) - 127.0), 8, axis=1)[..., None]
    return vals.transpose(0, 1, 3, 2).reshape(g * 512, n)


def sigmoid(v):
    return 1.0 / (1.0 + np.exp(-v))


def bf(x):
    return np.asarray(x, np.float32).astype(ml_dtypes.bfloat16)


def planes(Y):
    r, m = Y.shape
    b = f64(bf(Y)).reshape(r // 32, 32, m)
    amax = np.abs(b).max(1)
    byte = np.clip(np.where(amax > 0, np.frexp(amax)[1] - 1 + 127 - 7, 1), 1, 254)
    codes = (b * np.exp2(127.0 - byte)[:, None, :]).reshape(r, m).astype(np.float32).astype(ml_dtypes.float8_e4m3fn).view(np.uint8)
    words = codes.reshape(r // 512, 128, 4, m).transpose(0, 1, 3, 2)
    return np.ascontiguousarray(words), np.ascontiguousarray(byte.astype(np.uint8).reshape(r // 512, 16, m))


D, T, I, Q, E, U, Z, M, C = 512, 2048, 512, 256, 512, 1024, 1024, 1024, 512


def setup_inputs():
    n = np.random.standard_normal
    idx = np.random.permutation(T)[:I]
    idx2 = np.random.permutation(U)[:I]
    idx3 = np.random.permutation(Z)[:I]
    idx4 = np.random.permutation(M)[:Q]
    fd = mx_kscale(D)
    fi = mx_kscale(I)
    fc = mx_kscale(C)
    ti = np.ones(T)
    ti[idx] = fi
    keysp = pack_weight(n((D, T)) / fd[:, None], "e2m1")
    return {
        "query": (n((D, Q)) * 0.6 / np.sqrt(D) * fd[:, None]).astype(np.float32),
        "query2": (n((D, Q)) * 0.6 / np.sqrt(D) * fd[:, None]).astype(np.float32),
        "query3": (n((D, Q)) * 0.6 / np.sqrt(D) * fd[:, None]).astype(np.float32),
        "keys_words": keysp[0],
        "keys_scales": keysp[1],
        "notes": (n((D, U)) / fd[:, None]).astype(np.float32),
        "pages": (n((D, Z)) / fd[:, None]).astype(np.float32),
        "os": (np.random.uniform(0.02, 0.08, (1, I)) * fi).astype(np.float32),
        "vals": (n((E, T)) / ti).astype(np.float32),
        "wm": (n((C, E)) * 1.0 / np.sqrt(C) * fc[:, None]).astype(np.float32),
        "mstore": (n((C, M)) / fc[:, None]).astype(np.float32),
        "offs": striped(idx),
        "offs2": striped(idx2),
        "offs3": striped(idx3),
        "offs4": striped(idx4),
    }


def reference(query, query2, query3, keys_words, keys_scales, notes, pages, os, vals, wm, mstore, offs, offs2, offs3, offs4):
    idx = unstriped(offs)
    idx2 = unstriped(offs2)
    idx3 = unstriped(offs3)
    idx4 = unstriped(offs4)
    keysu = unpack_weight(keys_words, keys_scales, "e2m1")
    queryq = mxq(f64(query), 0, "e4m3")
    keysidxg = keysu[:, idx]
    query2q = mxq(f64(query2), 0, "e4m3")
    notesidx2q = mxq(f64(notes)[:, idx2], 0, "e4m3")
    query3q = mxq(f64(query3), 0, "e4m3")
    pagesidx3q = mxq(f64(pages)[:, idx3], 0, "e4m3")
    s = queryq.T @ keysidxg + query2q.T @ notesidx2q + query3q.T @ pagesidx3q
    w = sigmoid(s)
    wo1 = w * f64(os)
    wt1 = wo1.T
    vt1 = f64(vals)[:, idx].T
    vt1q = mxq(vt1, 0, "e4m3")
    wt1q = mxq(wt1, 0, "e4m3")
    o = vt1q.T @ wt1q
    wmq = mxq(f64(wm), 0, "e4m3")
    mstoreq = mxq(f64(mstore), 0, "e4m3")
    me = wmq.T @ mstoreq
    y = np.maximum(o, me[:, idx4])
    words, scales = planes(y)
    return y, words, scales

@@ -1,0 +1,257 @@
+from contextlib import ExitStack
+
+import concourse.mybir as mybir
+from concourse.masks import make_identity
+
+D, T, I, Q, E, U, Z, M, C = 512, 2048, 512, 256, 512, 1024, 1024, 1024, 512
+FLOPS = 2 * (3 * D * Q * I + I * E * Q + C * E * M)
+
+F32 = mybir.dt.float32
+BF16 = mybir.dt.bfloat16
+I32 = mybir.dt.int32
+U32 = mybir.dt.uint32
+U16 = mybir.dt.uint16
+U8 = mybir.dt.uint8
+FP8X4 = mybir.dt.float8_e4m3fn_x4
+FP4X4 = mybir.dt.float4_e2m1fn_x4
+COPY = mybir.ActivationFunctionType.Copy
+SIGMOID = mybir.ActivationFunctionType.Sigmoid
+MULT = mybir.AluOpType.mult
+MAX = mybir.AluOpType.max
+
+P = 128
+PACK = 4
+HALF_M = M // 2
+HALF_Q = Q // 2
+
+
+def tile_attend_threesources_memorylarger_lean_pl_kernel(
+    tc, query, query2, query3, keys_words, keys_scales, notes, pages, factors, vals, wm, mstore,
+    offs, offs2, offs3, offs4, out_0, out_1, out_2,
+):
+    nc = tc.nc
+    with ExitStack() as ctx:
+        sb = ctx.enter_context(tc.tile_pool(name="sb", bufs=1))
+        late = ctx.enter_context(tc.tile_pool(name="late", bufs=1))
+        ps = ctx.enter_context(tc.psum_pool(name="ps", bufs=1))
+
+        def tile(shape, dtype, name):
+            return sb.tile(shape, dtype, name=name, align_bytes=64)
+
+        def load(shape, dtype, name, source):
+            loaded = tile(shape, dtype, name)
+            nc.sync.dma_start(out=loaded[:], in_=source)
+            return loaded
+
+        def rows_by_place(matrix):
+            return matrix.rearrange("(p j) w -> p j w", j=PACK)
+
+        def quantize(grouped, name):
+            width = grouped.shape[1] // PACK
+            codes = tile([P, width], U32, name + "_codes")
+            scales = tile([P, width], U8, name + "_scales")
+            nc.vector.quantize_mx(out=codes[:].bitcast(FP8X4), scales=scales[:], in_=grouped)
+            return codes, scales
+
+        def interleave(raw, name, copy=nc.vector.tensor_copy):
+            width = raw.shape[2]
+            grouped = tile([P, width * PACK], BF16, name + "_grouped")
+            copy(
+                out=grouped[:].rearrange("p (c i j) -> p c j i", i=4, j=PACK),
+                in_=raw[:].rearrange("p j (c i) -> p c j i", i=4),
+            )
+            return grouped
+
+        def interleave_dealt(raw, name):
+            grouped = tile([P, PACK * P * PACK], BF16, name + "_grouped")
+            nc.vector.tensor_copy(
+                out=grouped[:].rearrange("p (r s j) -> p s j r", r=PACK, j=PACK),
+                in_=raw[:].rearrange("p j (s r) -> p s j r", r=PACK),
+            )
+            return grouped
+
+        key_scale_pool = tile([P, T], U8, "key_scale_pool")
+        nc.gpsimd.memset(key_scale_pool[:].bitcast(I32), 0)
+        identity = tile([P, P], F32, "identity")
+        make_identity(nc, identity[:])
+
+        def load_list(source, name):
+            offsets = sb.tile(list(source.shape), U16, name=name)
+            nc.sync.dma_start(offsets[:], source)
+            return offsets
+
+        def load_place(matrix, j, name):
+            return load([P, matrix.shape[1]], F32, "%s%d" % (name, j), rows_by_place(matrix)[:, j, :])
+
+        note_pool = [None] * PACK
+        store_raw = [None] * 2
+        wm_raw = load([P, PACK, E], F32, "wm_raw", rows_by_place(wm))
+        note_pool[0] = load_place(notes, 0, "note_pool")
+        note_list = load_list(offs2, "note_list")
+        token_list = load_list(offs, "token_list")
+        store_raw[0] = load([P, PACK, HALF_M], F32, "store_raw0", rows_by_place(mstore)[:, :, :HALF_M])
+        note_pool[1] = load_place(notes, 1, "note_pool")
+        key_word_pool = tile([P, T], U16, "key_word_pool")
+        nc.sync.dma_start(out=key_word_pool[:].bitcast(I32), in_=keys_words[0].bitcast(I32))
+        for quad in range(4):
+            nc.sync.dma_start(
+                out=key_scale_pool[32 * quad : 32 * quad + 4, :].bitcast(I32),
+                in_=keys_scales[0, 4 * quad : 4 * quad + 4, :].bitcast(I32),
+            )
+        note_pool[2] = load_place(notes, 2, "note_pool")
+        store_raw[1] = load([P, PACK, HALF_M], F32, "store_raw1", rows_by_place(mstore)[:, :, HALF_M:])
+        note_pool[3] = load_place(notes, 3, "note_pool")
+        page_list = load_list(offs3, "page_list")
+        memory_list = load_list(offs4, "memory_list")
+        slot_factor = load([P, PACK], F32, "slot_factor", factors.rearrange("o (s r) -> (o s) r", r=PACK))
+        page_pool = [load_place(pages, j, "page_pool") for j in range(PACK)]
+        query_raw = [
+            load([P, PACK, Q], F32, "query_raw%d" % n, rows_by_place(rows))
+            for n, rows in enumerate((query, query2, query3))
+        ]
+        val_pool = [load_place(vals, j, "val_pool") for j in range(PACK - 1)]
+        last_pool = late.tile([P, T], F32, name="last_val_pool", offset=0, align_bytes=64)
+        nc.sync.dma_start(out=last_pool[:], in_=rows_by_place(vals)[:, PACK - 1, :])
+        val_pool.append(last_pool)
+
+        note_picked = tile([P, PACK, I], BF16, "note_picked")
+        page_picked = tile([P, PACK, I], BF16, "page_picked")
+
+        def pick(picked, pool, offsets, j):
+            nc.scalar.activation(picked[:, j, :], pool[j][:].indirect(offsets[:]), COPY)
+
+        def pick_on_vector(picked, pool, offsets, j):
+            nc.vector.tensor_copy(picked[:, j, :], pool[j][:].indirect(offsets[:]))
+
+        memory = [tile([P, M], F32, "memory%d" % j) for j in range(PACK)]
+
+        def make_memories(half, wm_q, store_q):
+            for j in range(PACK):
+                bank = ps.tile([P, HALF_M], F32, name="memory_bank", tag="memory_bank", bufs=3)
+                cols = slice(j * P, (j + 1) * P)
+                nc.tensor.matmul_mx(
+                    out=bank[:], lhsT=wm_q[0][:, cols].bitcast(FP8X4), lhsT_scale=wm_q[1][:, cols],
+                    rhs=store_q[0][:].bitcast(FP8X4), rhs_scale=store_q[1][:], start=True, stop=True,
+                )
+                nc.scalar.copy(memory[j][:, half * HALF_M : (half + 1) * HALF_M], bank[:])
+
+        scores = [ps.tile([P, PACK, HALF_Q], F32, name="scores%d" % h) for h in range(2)]
+
+        def score_passes(codes, fmt, scales, rows_q, first, last):
+            for h in range(2):
+                rows = slice(h * HALF_Q, (h + 1) * HALF_Q)
+                for r in range(PACK):
+                    cols = slice(r * P, (r + 1) * P)
+                    nc.tensor.matmul_mx(
+                        out=scores[h][:, r, :], lhsT=codes[:, cols].bitcast(fmt), lhsT_scale=scales[:, cols],
+                        rhs=rows_q[0][:, rows].bitcast(FP8X4), rhs_scale=rows_q[1][:, rows],
+                        start=(first and r == 0), stop=(last and r == PACK - 1),
+                    )
+
+        wm_q = quantize(interleave_dealt(wm_raw, "wm")[:], "wm")
+        pick(note_picked, note_pool, note_list, 0)
+        store_q0 = quantize(interleave(store_raw[0], "store0")[:], "store0")
+        pick(note_picked, note_pool, note_list, 1)
+        key_picked = tile([P, I], U16, "key_picked")
+        nc.vector.tensor_copy(key_picked[:], key_word_pool[:].indirect(token_list[:]))
+        key_words = tile([P, I], U16, "key_words")
+        nc.vector.tensor_copy(
+            key_words[:].rearrange("p (r s) -> p r s", r=PACK), key_picked[:].rearrange("p (s r) -> p r s", r=PACK)
+        )
+        key_scales = tile([P, I], U8, "key_scales")
+        nc.vector.tensor_copy(
+            key_scales[:].rearrange("p (r s) -> p s r", r=PACK), key_scale_pool[:].indirect(token_list[:])
+        )
+        make_memories(0, wm_q, store_q0)
+        pick(note_picked, note_pool, note_list, 2)
+        store_q1 = quantize(interleave(store_raw[1], "store1")[:], "store1")
+        pick(note_picked, note_pool, note_list, 3)
+        note_q = quantize(interleave_dealt(note_picked, "note")[:], "note")
+        pick(page_picked, page_pool, page_list, 0)
+        pick_on_vector(page_picked, page_pool, page_list, 1)
+        make_memories(1, wm_q, store_q1)
+        pick(page_picked, page_pool, page_list, 2)
+        pick_on_vector(page_picked, page_pool, page_list, 3)
+        page_q = quantize(interleave_dealt(page_picked, "page")[:], "page")
+        query_q = quantize(interleave(query_raw[0], "query0", nc.scalar.copy)[:], "query0")
+        score_passes(key_words, FP4X4, key_scales, query_q, True, False)
+        query_q = quantize(interleave(query_raw[1], "query1", nc.scalar.copy)[:], "query1")
+        score_passes(note_q[0], FP8X4, note_q[1], query_q, False, False)
+        query_q = quantize(interleave(query_raw[2], "query2")[:], "query2")
+        score_passes(page_q[0], FP8X4, page_q[1], query_q, False, True)
+
+        weight_codes = tile([P, Q], U32, "weight_codes")
+        weight_scales = tile([P, Q], U8, "weight_scales")
+        weight_grouped = []
+        for h in range(2):
+            weights = tile([P, HALF_Q, PACK], F32, "weights%d" % h)
+            nc.scalar.activation(weights[:], scores[h][:].rearrange("p r q -> p q r"), SIGMOID)
+            grouped = tile([P, HALF_Q, PACK], BF16, "weight_grouped%d" % h)
+            nc.vector.tensor_tensor(
+                grouped[:], weights[:], slot_factor[:].unsqueeze(1).to_broadcast([P, HALF_Q, PACK]), MULT
+            )
+            weight_grouped.append(grouped)
+        for h in range(2):
+            rows = slice(h * HALF_Q, (h + 1) * HALF_Q)
+            nc.vector.quantize_mx(
+                out=weight_codes[:, rows].bitcast(FP8X4), scales=weight_scales[:, rows],
+                in_=weight_grouped[h][:].rearrange("p q r -> p (q r)"),
+            )
+
+        memory_picked = sb.tile([P, PACK, Q], F32, name="memory_picked", tag="query_raw1", align_bytes=64)
+        for j in range(PACK):
+            nc.scalar.activation(memory_picked[:, j, :], memory[j][:].indirect(memory_list[:]), COPY)
+
+        val_picked = [tile([P, I], BF16, "val_picked%d" % j) for j in range(PACK)]
+        reads = [None] * PACK
+
+        def turn(j):
+            pairs = val_picked[j][:].bitcast(F32)
+            turned = ps.tile([P, 2, P], F32, name="turned", tag="turned", bufs=2)
+            for u in range(2):
+                nc.tensor.transpose(turned[:, u, :], pairs[:, u::2], identity[:])
+            return turned
+
+        def read_values(j, turned, val_grouped, copy):
+            copy(val_grouped[:].bitcast(F32).rearrange("p (e u) -> p e u", u=2), turned[:].rearrange("p u e -> p e u"))
+            val_q = quantize(val_grouped[:], "val%d" % j)
+            if j < PACK - 1:
+                reads[j] = ps.tile([P, Q], F32, name="read", tag="memory_bank", bufs=3)
+            else:
+                reads[j] = ps.tile([P, Q], F32, name="last_read")
+            nc.tensor.matmul_mx(
+                out=reads[j][:], lhsT=val_q[0][:].bitcast(FP8X4), lhsT_scale=val_q[1][:],
+                rhs=weight_codes[:].bitcast(FP8X4), rhs_scale=weight_scales[:], start=True, stop=True,
+            )
+
+        def hand_out(j):
+            nc.vector.tensor_tensor(result[:, j, :], reads[j][:], memory_picked[:, j, :], MAX)
+            nc.sync.dma_start(out=rows_by_place(out_0)[:, j, :], in_=result[:, j, :])
+
+        nc.vector.tensor_copy(val_picked[0][:], val_pool[0][:].indirect(token_list[:]))
+        read_values(0, turn(0), tile([P, P * PACK], BF16, "val_grouped0"), nc.scalar.copy)
+        nc.scalar.activation(val_picked[1][:], val_pool[1][:].indirect(token_list[:]), COPY)
+        read_values(1, turn(1), tile([P, P * PACK], BF16, "val_grouped1"), nc.vector.tensor_copy)
+        nc.scalar.activation(val_picked[2][:], val_pool[2][:].indirect(token_list[:]), COPY)
+        turned2 = turn(2)
+        half = I // 2
+        nc.vector.tensor_copy(val_picked[3][:, :half], val_pool[3][:].indirect(token_list[:, : half // 16]))
+        nc.scalar.activation(val_picked[3][:, half:], val_pool[3][:].indirect(token_list[:, half // 16 :]), COPY)
+        result = late.tile([P, PACK, Q], F32, name="result", offset=0, align_bytes=64)
+        val_grouped2 = late.tile([P, P * PACK], BF16, name="val_grouped2", offset=PACK * Q * 4, align_bytes=64)
+        read_values(2, turned2, val_grouped2, nc.vector.tensor_copy)
+        for j in range(PACK - 1):
+            hand_out(j)
+        read_values(3, turn(3), tile([P, P * PACK], BF16, "val_grouped3"), nc.scalar.copy)
+        hand_out(3)
+
+        result_q = quantize(interleave(result, "result")[:], "result")
+        nc.sync.dma_start(
+            out=out_1[0].rearrange("p q r -> p (q r)").bitcast(I32), in_=result_q[0][:].bitcast(I32)
+        )
+        for quad in range(4):
+            engine = nc.sync if quad % 2 == 0 else nc.scalar
+            engine.dma_start(
+                out=out_2[0, 4 * quad : 4 * quad + 4, :].bitcast(I32),
+                in_=result_q[1][32 * quad : 32 * quad + 4, :].bitcast(I32),
+            )

@@ -84,22 +84,22 @@ def tile_attend_threesources_memorylarger_lean_pl_kernel(
             return load([P, matrix.shape[1]], F32, "%s%d" % (name, j), rows_by_place(matrix)[:, j, :])
 
         note_pool = [None] * PACK
-        store_raw = [None] * 2
         wm_raw = load([P, PACK, E], F32, "wm_raw", rows_by_place(wm))
         note_pool[0] = load_place(notes, 0, "note_pool")
         note_list = load_list(offs2, "note_list")
         token_list = load_list(offs, "token_list")
-        store_raw[0] = load([P, PACK, HALF_M], F32, "store_raw0", rows_by_place(mstore)[:, :, :HALF_M])
-        note_pool[1] = load_place(notes, 1, "note_pool")
+        store_raw = [
+            load([P, PACK, HALF_M], F32, "store_raw%d" % h, rows_by_place(mstore)[:, :, h * HALF_M : (h + 1) * HALF_M])
+            for h in range(2)
+        ]
         key_word_pool = tile([P, T], U16, "key_word_pool")
         nc.sync.dma_start(out=key_word_pool[:].bitcast(I32), in_=keys_words[0].bitcast(I32))
-        for quad in range(4):
+        note_pool[1] = load_place(notes, 1, "note_pool")
+        for row in range(4):
             nc.sync.dma_start(
-                out=key_scale_pool[32 * quad : 32 * quad + 4, :].bitcast(I32),
-                in_=keys_scales[0, 4 * quad : 4 * quad + 4, :].bitcast(I32),
+                out=key_scale_pool[row:P:32, :].bitcast(I32), in_=keys_scales[0, row:16:4, :].bitcast(I32)
             )
         note_pool[2] = load_place(notes, 2, "note_pool")
-        store_raw[1] = load([P, PACK, HALF_M], F32, "store_raw1", rows_by_place(mstore)[:, :, HALF_M:])
         note_pool[3] = load_place(notes, 3, "note_pool")
         page_list = load_list(offs3, "page_list")
         memory_list = load_list(offs4, "memory_list")
@@ -150,7 +150,8 @@ def tile_attend_threesources_memorylarger_lean_pl_kernel(
 
         wm_q = quantize(interleave_dealt(wm_raw, "wm")[:], "wm")
         pick(note_picked, note_pool, note_list, 0)
-        store_q0 = quantize(interleave(store_raw[0], "store0")[:], "store0")
+        store_q = [quantize(interleave(store_raw[h], "store%d" % h)[:], "store%d" % h) for h in range(2)]
+        make_memories(0, wm_q, store_q[0])
         pick(note_picked, note_pool, note_list, 1)
         key_picked = tile([P, I], U16, "key_picked")
         nc.vector.tensor_copy(key_picked[:], key_word_pool[:].indirect(token_list[:]))
@@ -162,15 +163,13 @@ def tile_attend_threesources_memorylarger_lean_pl_kernel(
         nc.vector.tensor_copy(
             key_scales[:].rearrange("p (r s) -> p s r", r=PACK), key_scale_pool[:].indirect(token_list[:])
         )
-        make_memories(0, wm_q, store_q0)
-        pick(note_picked, note_pool, note_list, 2)
-        store_q1 = quantize(interleave(store_raw[1], "store1")[:], "store1")
-        pick(note_picked, note_pool, note_list, 3)
+        make_memories(1, wm_q, store_q[1])
+        pick_on_vector(note_picked, note_pool, note_list, 2)
+        pick_on_vector(note_picked, note_pool, note_list, 3)
         note_q = quantize(interleave_dealt(note_picked, "note")[:], "note")
         pick(page_picked, page_pool, page_list, 0)
-        pick_on_vector(page_picked, page_pool, page_list, 1)
-        make_memories(1, wm_q, store_q1)
-        pick(page_picked, page_pool, page_list, 2)
+        pick(page_picked, page_pool, page_list, 1)
+        pick_on_vector(page_picked, page_pool, page_list, 2)
         pick_on_vector(page_picked, page_pool, page_list, 3)
         page_q = quantize(interleave_dealt(page_picked, "page")[:], "page")
         query_q = quantize(interleave(query_raw[0], "query0", nc.scalar.copy)[:], "query0")
@@ -198,9 +197,12 @@ def tile_attend_threesources_memorylarger_lean_pl_kernel(
                 in_=weight_grouped[h][:].rearrange("p q r -> p (q r)"),
             )
 
-        memory_picked = sb.tile([P, PACK, Q], F32, name="memory_picked", tag="query_raw1", align_bytes=64)
+        memory_picked = []
+        for tag in ("page_pool1", "query_raw1"):
+            pair = sb.tile([P, 2, Q], F32, name="memory_picked_on_" + tag, tag=tag, align_bytes=64)
+            memory_picked.extend([pair[:, 0, :], pair[:, 1, :]])
         for j in range(PACK):
-            nc.scalar.activation(memory_picked[:, j, :], memory[j][:].indirect(memory_list[:]), COPY)
+            nc.scalar.activation(memory_picked[j], memory[j][:].indirect(memory_list[:]), COPY)
 
         val_picked = [tile([P, I], BF16, "val_picked%d" % j) for j in range(PACK)]
         reads = [None] * PACK
@@ -225,7 +227,7 @@ def tile_attend_threesources_memorylarger_lean_pl_kernel(
             )
 
         def hand_out(j):
-            nc.vector.tensor_tensor(result[:, j, :], reads[j][:], memory_picked[:, j, :], MAX)
+            nc.vector.tensor_tensor(result[:, j, :], reads[j][:], memory_picked[j], MAX)
             nc.sync.dma_start(out=rows_by_place(out_0)[:, j, :], in_=result[:, j, :])
 
         nc.vector.tensor_copy(val_picked[0][:], val_pool[0][:].indirect(token_list[:]))

@@ -70,6 +70,11 @@ def tile_attend_threesources_memorylarger_lean_pl_kernel(
             )
             return grouped
 
+        warm_in = tile([P, 1], F32, "warm_in")
+        warm_out = tile([P, 1], F32, "warm_out")
+        nc.vector.memset(warm_in[:], 0.0)
+        nc.scalar.activation(warm_out[:], warm_in[:], SIGMOID)
+
         key_scale_pool = tile([P, T], U8, "key_scale_pool")
         nc.gpsimd.memset(key_scale_pool[:].bitcast(I32), 0)
         identity = tile([P, P], F32, "identity")

@@ -101,14 +101,15 @@ def tile_attend_threesources_memorylarger_lean_pl_kernel(
         nc.sync.dma_start(out=key_word_pool[:].bitcast(I32), in_=keys_words[0].bitcast(I32))
         note_pool[1] = load_place(notes, 1, "note_pool")
         for row in range(4):
-            nc.sync.dma_start(
+            nc.scalar.dma_start(
                 out=key_scale_pool[row:P:32, :].bitcast(I32), in_=keys_scales[0, row:16:4, :].bitcast(I32)
             )
         note_pool[2] = load_place(notes, 2, "note_pool")
         note_pool[3] = load_place(notes, 3, "note_pool")
         page_list = load_list(offs3, "page_list")
         memory_list = load_list(offs4, "memory_list")
-        slot_factor = load([P, PACK], F32, "slot_factor", factors.rearrange("o (s r) -> (o s) r", r=PACK))
+        slot_factor = tile([P, PACK], F32, "slot_factor")
+        nc.scalar.dma_start(out=slot_factor[:], in_=factors.rearrange("o (s r) -> (o s) r", r=PACK))
         page_pool = [load_place(pages, j, "page_pool") for j in range(PACK)]
         query_raw = [
             load([P, PACK, Q], F32, "query_raw%d" % n, rows_by_place(rows))
@@ -246,13 +247,19 @@ def tile_attend_threesources_memorylarger_lean_pl_kernel(
         nc.scalar.activation(val_picked[3][:, half:], val_pool[3][:].indirect(token_list[:, half // 16 :]), COPY)
         result = late.tile([P, PACK, Q], F32, name="result", offset=0, align_bytes=64)
         val_grouped2 = late.tile([P, P * PACK], BF16, name="val_grouped2", offset=PACK * Q * 4, align_bytes=64)
-        read_values(2, turned2, val_grouped2, nc.vector.tensor_copy)
+        read_values(2, turned2, val_grouped2, nc.scalar.copy)
         for j in range(PACK - 1):
             hand_out(j)
         read_values(3, turn(3), tile([P, P * PACK], BF16, "val_grouped3"), nc.scalar.copy)
         hand_out(3)
 
-        result_q = quantize(interleave(result, "result")[:], "result")
+        result_grouped = tile([P, Q * PACK], BF16, "result_grouped")
+        for first, copy in ((0, nc.scalar.copy), (2, nc.vector.tensor_copy)):
+            copy(
+                result_grouped[:].rearrange("p (q j) -> p q j", j=PACK)[:, :, first : first + 2],
+                result[:, first : first + 2, :].rearrange("p j q -> p q j"),
+            )
+        result_q = quantize(result_grouped[:], "result")
         nc.sync.dma_start(
             out=out_1[0].rearrange("p q r -> p (q r)").bitcast(I32), in_=result_q[0][:].bitcast(I32)
         )

@@ -220,17 +220,20 @@ def tile_attend_threesources_memorylarger_lean_pl_kernel(
                 nc.tensor.transpose(turned[:, u, :], pairs[:, u::2], identity[:])
             return turned
 
-        def read_values(j, turned, val_grouped, copy):
+        def quantize_values(j, turned, val_grouped, copy):
             copy(val_grouped[:].bitcast(F32).rearrange("p (e u) -> p e u", u=2), turned[:].rearrange("p u e -> p e u"))
-            val_q = quantize(val_grouped[:], "val%d" % j)
-            if j < PACK - 1:
-                reads[j] = ps.tile([P, Q], F32, name="read", tag="memory_bank", bufs=3)
-            else:
-                reads[j] = ps.tile([P, Q], F32, name="last_read")
+            return quantize(val_grouped[:], "val%d" % j)
+
+        def read_rows(bank, val_q, rows):
             nc.tensor.matmul_mx(
-                out=reads[j][:], lhsT=val_q[0][:].bitcast(FP8X4), lhsT_scale=val_q[1][:],
-                rhs=weight_codes[:].bitcast(FP8X4), rhs_scale=weight_scales[:], start=True, stop=True,
+                out=bank[:], lhsT=val_q[0][:].bitcast(FP8X4), lhsT_scale=val_q[1][:],
+                rhs=weight_codes[:, rows].bitcast(FP8X4), rhs_scale=weight_scales[:, rows], start=True, stop=True,
             )
+
+        def read_values(j, turned, val_grouped, copy):
+            val_q = quantize_values(j, turned, val_grouped, copy)
+            reads[j] = ps.tile([P, Q], F32, name="read", tag="memory_bank", bufs=3)
+            read_rows(reads[j], val_q, slice(0, Q))
 
         def hand_out(j):
             nc.vector.tensor_tensor(result[:, j, :], reads[j][:], memory_picked[j], MAX)
@@ -250,19 +253,28 @@ def tile_attend_threesources_memorylarger_lean_pl_kernel(
         read_values(2, turned2, val_grouped2, nc.scalar.copy)
         for j in range(PACK - 1):
             hand_out(j)
-        read_values(3, turn(3), tile([P, P * PACK], BF16, "val_grouped3"), nc.scalar.copy)
-        hand_out(3)
+        last_q = quantize_values(3, turn(3), tile([P, P * PACK], BF16, "val_grouped3"), nc.scalar.copy)
+        halves = [slice(h * HALF_Q, (h + 1) * HALF_Q) for h in range(2)]
+        for h, rows in enumerate(halves):
+            last_read = ps.tile([P, HALF_Q], F32, name="last_read%d" % h, tag="scores%d" % h)
+            read_rows(last_read, last_q, rows)
+            nc.vector.tensor_tensor(result[:, 3, rows], last_read[:], memory_picked[3][:, rows], MAX)
+        nc.sync.dma_start(out=rows_by_place(out_0)[:, 3, :], in_=result[:, 3, :])
 
-        result_grouped = tile([P, Q * PACK], BF16, "result_grouped")
-        for first, copy in ((0, nc.scalar.copy), (2, nc.vector.tensor_copy)):
-            copy(
-                result_grouped[:].rearrange("p (q j) -> p q j", j=PACK)[:, :, first : first + 2],
-                result[:, first : first + 2, :].rearrange("p j q -> p q j"),
+        result_grouped = tile([P, Q, PACK], BF16, "result_grouped")
+        nc.scalar.copy(result_grouped[:, :, 0:2], result[:, 0:2, :].rearrange("p j q -> p q j"))
+        for rows in halves:
+            nc.vector.tensor_copy(result_grouped[:, rows, 2:4], result[:, 2:4, rows].rearrange("p j q -> p q j"))
+        result_q = (tile([P, Q], U32, "result_codes"), tile([P, Q], U8, "result_scales"))
+        for rows in halves:
+            nc.vector.quantize_mx(
+                out=result_q[0][:, rows].bitcast(FP8X4), scales=result_q[1][:, rows],
+                in_=result_grouped[:, rows, :].rearrange("p q j -> p (q j)"),
             )
-        result_q = quantize(result_grouped[:], "result")
-        nc.sync.dma_start(
-            out=out_1[0].rearrange("p q r -> p (q r)").bitcast(I32), in_=result_q[0][:].bitcast(I32)
-        )
+            nc.sync.dma_start(
+                out=out_1[0, :, rows, :].rearrange("p q r -> p (q r)").bitcast(I32),
+                in_=result_q[0][:, rows].bitcast(I32),
+            )
         for quad in range(4):
             engine = nc.sync if quad % 2 == 0 else nc.scalar
             engine.dma_start(

from contextlib import ExitStack

import concourse.mybir as mybir
from concourse.masks import make_identity

D, T, I, Q, E, U, Z, M, C = 512, 2048, 512, 256, 512, 1024, 1024, 1024, 512
FLOPS = 2 * (3 * D * Q * I + I * E * Q + C * E * M)

F32 = mybir.dt.float32
BF16 = mybir.dt.bfloat16
I32 = mybir.dt.int32
U32 = mybir.dt.uint32
U16 = mybir.dt.uint16
U8 = mybir.dt.uint8
FP8X4 = mybir.dt.float8_e4m3fn_x4
FP4X4 = mybir.dt.float4_e2m1fn_x4
COPY = mybir.ActivationFunctionType.Copy
SIGMOID = mybir.ActivationFunctionType.Sigmoid
MULT = mybir.AluOpType.mult
MAX = mybir.AluOpType.max

P = 128
PACK = 4
HALF_M = M // 2
HALF_Q = Q // 2


def tile_attend_threesources_memorylarger_lean_pl_kernel(
    tc, query, query2, query3, keys_words, keys_scales, notes, pages, factors, vals, wm, mstore,
    offs, offs2, offs3, offs4, out_0, out_1, out_2,
):
    nc = tc.nc
    with ExitStack() as ctx:
        sb = ctx.enter_context(tc.tile_pool(name="sb", bufs=1))
        late = ctx.enter_context(tc.tile_pool(name="late", bufs=1))
        ps = ctx.enter_context(tc.psum_pool(name="ps", bufs=1))

        def tile(shape, dtype, name):
            return sb.tile(shape, dtype, name=name, align_bytes=64)

        def load(shape, dtype, name, source):
            loaded = tile(shape, dtype, name)
            nc.sync.dma_start(out=loaded[:], in_=source)
            return loaded

        def rows_by_place(matrix):
            return matrix.rearrange("(p j) w -> p j w", j=PACK)

        def quantize(grouped, name):
            width = grouped.shape[1] // PACK
            codes = tile([P, width], U32, name + "_codes")
            scales = tile([P, width], U8, name + "_scales")
            nc.vector.quantize_mx(out=codes[:].bitcast(FP8X4), scales=scales[:], in_=grouped)
            return codes, scales

        def interleave(raw, name, copy=nc.vector.tensor_copy):
            width = raw.shape[2]
            grouped = tile([P, width * PACK], BF16, name + "_grouped")
            copy(
                out=grouped[:].rearrange("p (c i j) -> p c j i", i=4, j=PACK),
                in_=raw[:].rearrange("p j (c i) -> p c j i", i=4),
            )
            return grouped

        def interleave_dealt(raw, name):
            grouped = tile([P, PACK * P * PACK], BF16, name + "_grouped")
            nc.vector.tensor_copy(
                out=grouped[:].rearrange("p (r s j) -> p s j r", r=PACK, j=PACK),
                in_=raw[:].rearrange("p j (s r) -> p s j r", r=PACK),
            )
            return grouped

        warm_in = tile([P, 1], F32, "warm_in")
        warm_out = tile([P, 1], F32, "warm_out")
        nc.vector.memset(warm_in[:], 0.0)
        nc.scalar.activation(warm_out[:], warm_in[:], SIGMOID)

        key_scale_pool = tile([P, T], U8, "key_scale_pool")
        nc.gpsimd.memset(key_scale_pool[:].bitcast(I32), 0)
        identity = tile([P, P], F32, "identity")
        make_identity(nc, identity[:])

        def load_list(source, name):
            offsets = sb.tile(list(source.shape), U16, name=name)
            nc.sync.dma_start(offsets[:], source)
            return offsets

        def load_place(matrix, j, name):
            return load([P, matrix.shape[1]], F32, "%s%d" % (name, j), rows_by_place(matrix)[:, j, :])

        note_pool = [None] * PACK
        wm_raw = load([P, PACK, E], F32, "wm_raw", rows_by_place(wm))
        note_pool[0] = load_place(notes, 0, "note_pool")
        note_list = load_list(offs2, "note_list")
        token_list = load_list(offs, "token_list")
        store_raw = [
            load([P, PACK, HALF_M], F32, "store_raw%d" % h, rows_by_place(mstore)[:, :, h * HALF_M : (h + 1) * HALF_M])
            for h in range(2)
        ]
        key_word_pool = tile([P, T], U16, "key_word_pool")
        nc.sync.dma_start(out=key_word_pool[:].bitcast(I32), in_=keys_words[0].bitcast(I32))
        note_pool[1] = load_place(notes, 1, "note_pool")
        for row in range(4):
            nc.scalar.dma_start(
                out=key_scale_pool[row:P:32, :].bitcast(I32), in_=keys_scales[0, row:16:4, :].bitcast(I32)
            )
        note_pool[2] = load_place(notes, 2, "note_pool")
        note_pool[3] = load_place(notes, 3, "note_pool")
        page_list = load_list(offs3, "page_list")
        memory_list = load_list(offs4, "memory_list")
        slot_factor = tile([P, PACK], F32, "slot_factor")
        nc.scalar.dma_start(out=slot_factor[:], in_=factors.rearrange("o (s r) -> (o s) r", r=PACK))
        page_pool = [load_place(pages, j, "page_pool") for j in range(PACK)]
        query_raw = [
            load([P, PACK, Q], F32, "query_raw%d" % n, rows_by_place(rows))
            for n, rows in enumerate((query, query2, query3))
        ]
        val_pool = [load_place(vals, j, "val_pool") for j in range(PACK - 1)]
        last_pool = late.tile([P, T], F32, name="last_val_pool", offset=0, align_bytes=64)
        nc.sync.dma_start(out=last_pool[:], in_=rows_by_place(vals)[:, PACK - 1, :])
        val_pool.append(last_pool)

        note_picked = tile([P, PACK, I], BF16, "note_picked")
        page_picked = tile([P, PACK, I], BF16, "page_picked")

        def pick(picked, pool, offsets, j):
            nc.scalar.activation(picked[:, j, :], pool[j][:].indirect(offsets[:]), COPY)

        def pick_on_vector(picked, pool, offsets, j):
            nc.vector.tensor_copy(picked[:, j, :], pool[j][:].indirect(offsets[:]))

        memory = [tile([P, M], F32, "memory%d" % j) for j in range(PACK)]

        def make_memories(half, wm_q, store_q):
            for j in range(PACK):
                bank = ps.tile([P, HALF_M], F32, name="memory_bank", tag="memory_bank", bufs=3)
                cols = slice(j * P, (j + 1) * P)
                nc.tensor.matmul_mx(
                    out=bank[:], lhsT=wm_q[0][:, cols].bitcast(FP8X4), lhsT_scale=wm_q[1][:, cols],
                    rhs=store_q[0][:].bitcast(FP8X4), rhs_scale=store_q[1][:], start=True, stop=True,
                )
                nc.scalar.copy(memory[j][:, half * HALF_M : (half + 1) * HALF_M], bank[:])

        scores = [ps.tile([P, PACK, HALF_Q], F32, name="scores%d" % h) for h in range(2)]

        def score_passes(codes, fmt, scales, rows_q, first, last):
            for h in range(2):
                rows = slice(h * HALF_Q, (h + 1) * HALF_Q)
                for r in range(PACK):
                    cols = slice(r * P, (r + 1) * P)
                    nc.tensor.matmul_mx(
                        out=scores[h][:, r, :], lhsT=codes[:, cols].bitcast(fmt), lhsT_scale=scales[:, cols],
                        rhs=rows_q[0][:, rows].bitcast(FP8X4), rhs_scale=rows_q[1][:, rows],
                        start=(first and r == 0), stop=(last and r == PACK - 1),
                    )

        wm_q = quantize(interleave_dealt(wm_raw, "wm")[:], "wm")
        pick(note_picked, note_pool, note_list, 0)
        store_q = [quantize(interleave(store_raw[h], "store%d" % h)[:], "store%d" % h) for h in range(2)]
        make_memories(0, wm_q, store_q[0])
        pick(note_picked, note_pool, note_list, 1)
        key_picked = tile([P, I], U16, "key_picked")
        nc.vector.tensor_copy(key_picked[:], key_word_pool[:].indirect(token_list[:]))
        key_words = tile([P, I], U16, "key_words")
        nc.vector.tensor_copy(
            key_words[:].rearrange("p (r s) -> p r s", r=PACK), key_picked[:].rearrange("p (s r) -> p r s", r=PACK)
        )
        key_scales = tile([P, I], U8, "key_scales")
        nc.vector.tensor_copy(
            key_scales[:].rearrange("p (r s) -> p s r", r=PACK), key_scale_pool[:].indirect(token_list[:])
        )
        make_memories(1, wm_q, store_q[1])
        pick_on_vector(note_picked, note_pool, note_list, 2)
        pick_on_vector(note_picked, note_pool, note_list, 3)
        note_q = quantize(interleave_dealt(note_picked, "note")[:], "note")
        pick(page_picked, page_pool, page_list, 0)
        pick(page_picked, page_pool, page_list, 1)
        pick_on_vector(page_picked, page_pool, page_list, 2)
        pick_on_vector(page_picked, page_pool, page_list, 3)
        page_q = quantize(interleave_dealt(page_picked, "page")[:], "page")
        query_q = quantize(interleave(query_raw[0], "query0", nc.scalar.copy)[:], "query0")
        score_passes(key_words, FP4X4, key_scales, query_q, True, False)
        query_q = quantize(interleave(query_raw[1], "query1", nc.scalar.copy)[:], "query1")
        score_passes(note_q[0], FP8X4, note_q[1], query_q, False, False)
        query_q = quantize(interleave(query_raw[2], "query2")[:], "query2")
        score_passes(page_q[0], FP8X4, page_q[1], query_q, False, True)

        weight_codes = tile([P, Q], U32, "weight_codes")
        weight_scales = tile([P, Q], U8, "weight_scales")
        weight_grouped = []
        for h in range(2):
            weights = tile([P, HALF_Q, PACK], F32, "weights%d" % h)
            nc.scalar.activation(weights[:], scores[h][:].rearrange("p r q -> p q r"), SIGMOID)
            grouped = tile([P, HALF_Q, PACK], BF16, "weight_grouped%d" % h)
            nc.vector.tensor_tensor(
                grouped[:], weights[:], slot_factor[:].unsqueeze(1).to_broadcast([P, HALF_Q, PACK]), MULT
            )
            weight_grouped.append(grouped)
        for h in range(2):
            rows = slice(h * HALF_Q, (h + 1) * HALF_Q)
            nc.vector.quantize_mx(
                out=weight_codes[:, rows].bitcast(FP8X4), scales=weight_scales[:, rows],
                in_=weight_grouped[h][:].rearrange("p q r -> p (q r)"),
            )

        memory_picked = []
        for tag in ("page_pool1", "query_raw1"):
            pair = sb.tile([P, 2, Q], F32, name="memory_picked_on_" + tag, tag=tag, align_bytes=64)
            memory_picked.extend([pair[:, 0, :], pair[:, 1, :]])
        for j in range(PACK):
            nc.scalar.activation(memory_picked[j], memory[j][:].indirect(memory_list[:]), COPY)

        val_picked = [tile([P, I], BF16, "val_picked%d" % j) for j in range(PACK)]
        reads = [None] * PACK

        def turn(j):
            pairs = val_picked[j][:].bitcast(F32)
            turned = ps.tile([P, 2, P], F32, name="turned", tag="turned", bufs=2)
            for u in range(2):
                nc.tensor.transpose(turned[:, u, :], pairs[:, u::2], identity[:])
            return turned

        def quantize_values(j, turned, val_grouped, copy):
            copy(val_grouped[:].bitcast(F32).rearrange("p (e u) -> p e u", u=2), turned[:].rearrange("p u e -> p e u"))
            return quantize(val_grouped[:], "val%d" % j)

        def read_rows(bank, val_q, rows):
            nc.tensor.matmul_mx(
                out=bank[:], lhsT=val_q[0][:].bitcast(FP8X4), lhsT_scale=val_q[1][:],
                rhs=weight_codes[:, rows].bitcast(FP8X4), rhs_scale=weight_scales[:, rows], start=True, stop=True,
            )

        def read_values(j, turned, val_grouped, copy):
            val_q = quantize_values(j, turned, val_grouped, copy)
            reads[j] = ps.tile([P, Q], F32, name="read", tag="memory_bank", bufs=3)
            read_rows(reads[j], val_q, slice(0, Q))

        def hand_out(j):
            nc.vector.tensor_tensor(result[:, j, :], reads[j][:], memory_picked[j], MAX)
            nc.sync.dma_start(out=rows_by_place(out_0)[:, j, :], in_=result[:, j, :])

        nc.vector.tensor_copy(val_picked[0][:], val_pool[0][:].indirect(token_list[:]))
        read_values(0, turn(0), tile([P, P * PACK], BF16, "val_grouped0"), nc.scalar.copy)
        nc.scalar.activation(val_picked[1][:], val_pool[1][:].indirect(token_list[:]), COPY)
        read_values(1, turn(1), tile([P, P * PACK], BF16, "val_grouped1"), nc.vector.tensor_copy)
        nc.scalar.activation(val_picked[2][:], val_pool[2][:].indirect(token_list[:]), COPY)
        turned2 = turn(2)
        half = I // 2
        nc.vector.tensor_copy(val_picked[3][:, :half], val_pool[3][:].indirect(token_list[:, : half // 16]))
        nc.scalar.activation(val_picked[3][:, half:], val_pool[3][:].indirect(token_list[:, half // 16 :]), COPY)
        result = late.tile([P, PACK, Q], F32, name="result", offset=0, align_bytes=64)
        val_grouped2 = late.tile([P, P * PACK], BF16, name="val_grouped2", offset=PACK * Q * 4, align_bytes=64)
        read_values(2, turned2, val_grouped2, nc.scalar.copy)
        for j in range(PACK - 1):
            hand_out(j)
        last_q = quantize_values(3, turn(3), tile([P, P * PACK], BF16, "val_grouped3"), nc.scalar.copy)
        halves = [slice(h * HALF_Q, (h + 1) * HALF_Q) for h in range(2)]
        for h, rows in enumerate(halves):
            last_read = ps.tile([P, HALF_Q], F32, name="last_read%d" % h, tag="scores%d" % h)
            read_rows(last_read, last_q, rows)
            nc.vector.tensor_tensor(result[:, 3, rows], last_read[:], memory_picked[3][:, rows], MAX)
        nc.sync.dma_start(out=rows_by_place(out_0)[:, 3, :], in_=result[:, 3, :])

        result_grouped = tile([P, Q, PACK], BF16, "result_grouped")
        nc.scalar.copy(result_grouped[:, :, 0:2], result[:, 0:2, :].rearrange("p j q -> p q j"))
        for rows in halves:
            nc.vector.tensor_copy(result_grouped[:, rows, 2:4], result[:, 2:4, rows].rearrange("p j q -> p q j"))
        result_q = (tile([P, Q], U32, "result_codes"), tile([P, Q], U8, "result_scales"))
        for rows in halves:
            nc.vector.quantize_mx(
                out=result_q[0][:, rows].bitcast(FP8X4), scales=result_q[1][:, rows],
                in_=result_grouped[:, rows, :].rearrange("p q j -> p (q j)"),
            )
            nc.sync.dma_start(
                out=out_1[0, :, rows, :].rearrange("p q r -> p (q r)").bitcast(I32),
                in_=result_q[0][:, rows].bitcast(I32),
            )
        for quad in range(4):
            engine = nc.sync if quad % 2 == 0 else nc.scalar
            engine.dma_start(
                out=out_2[0, 4 * quad : 4 * quad + 4, :].bitcast(I32),
                in_=result_q[1][32 * quad : 32 * quad + 4, :].bitcast(I32),
            )
